import numpy as np
import ml_dtypes


def mxq(x, axis, fmt="e4m3"):
    dtype, down = {"e4m3": (ml_dtypes.float8_e4m3fn, 7), "e5m2": (ml_dtypes.float8_e5m2, 14)}[fmt]
    v = np.moveaxis(np.asarray(x, np.float32).astype(ml_dtypes.bfloat16).astype(np.float64), axis, -1)
    blocks = v.reshape(v.shape[:-1] + (-1, 32))
    amax = np.abs(blocks).max(-1, keepdims=True)
    byte = np.maximum(np.where(amax > 0, np.frexp(amax)[1] - 1 + 127, 0) - down, 1)
    scale = np.exp2(byte - 127.0)
    codes = (blocks / scale).astype(np.float32).astype(dtype).astype(np.float64)
    return np.moveaxis((codes * scale).reshape(v.shape), -1, axis)


WIDE = False


def mx_kscale(k):
    if not WIDE:
        return np.ones(k)
    levels = np.array([10, -10, 5, -5, 0])
    if k % 512:
        return np.exp2(np.random.permutation(np.resize(levels, k // 32))).repeat(32)
    a = np.empty((k // 512, 16))
    for p in range(k // 512):
        a[p, :8] = np.random.permutation(np.resize(levels, 8))
        for g in range(8):
            far = levels[np.abs(levels - a[p, g]) >= 10]
            a[p, g + 8] = far[np.random.randint(len(far))]
    return np.exp2(a.ravel()).repeat(32)


BF16 = ml_dtypes.bfloat16


def bf(x):
    return np.asarray(x, np.float32).astype(BF16)


def f64(x):
    return np.asarray(x).astype(np.float64)


E2M1 = np.array([0.0, 0.5, 1.0, 1.5, 2.0, 3.0, 4.0, 6.0, -0.0, -0.5, -1.0, -1.5, -2.0, -3.0, -4.0, -6.0])


def pack_weight(w, fmt):
    k, n = w.shape
    w = f64(bf(w)).reshape(k // 32, 32, n)
    amax = np.abs(w).max(1)
    if fmt == "e4m3":
        byte = np.frexp(amax)[1] - 1 + 127 - 7
    else:
        mant, ex = np.frexp(amax / 6.0)
        byte = np.where(mant > 0.5, ex, ex - 1) + 127
    byte = np.clip(np.where(amax > 0, byte, 1), 1, 254)
    scaled = (w * np.exp2(127.0 - byte)[:, None, :]).reshape(k, n).astype(np.float32)
    by_word = np.ascontiguousarray(scaled.reshape(k // 512, 128, 4, n).transpose(0, 1, 3, 2))
    if fmt == "e4m3":
        words = by_word.astype(ml_dtypes.float8_e4m3fn).view(np.uint8)
    else:
        c = by_word.astype(ml_dtypes.float4_e2m1fn).view(np.uint8) & 0xF
        words = c[..., 0::2] | (c[..., 1::2] << 4)
    return np.ascontiguousarray(words), np.ascontiguousarray(byte.astype(np.uint8).reshape(k // 512, 16, n))


def unpack_weight(words, scales, fmt):
    g, p, n, _ = words.shape
    if fmt == "e4m3":
        vals = np.ascontiguousarray(words).view(ml_dtypes.float8_e4m3fn).astype(np.float64)
    else:
        nib = np.empty((g, p, n, 4), np.uint8)
        nib[..., 0::2] = words & 0xF
        nib[..., 1::2] = words >> 4
        vals = E2M1[nib]
    vals = vals * np.repeat(np.exp2(scales.astype(np.float64) - 127.0), 8, axis=1)[..., None]
    return vals.transpose(0, 1, 3, 2).reshape(g * 512, n)
def pack4(w):
    words, scales = pack_weight(w, "e2m1")
    return words.reshape(words.shape[0], 128, -1), scales


def unpack4(words, scales):
    return unpack_weight(words.reshape(words.shape[0], 128, -1, 2), scales, "e2m1")


N, T, J = 1024, 1536, 512


def setup_inputs():
    s = mx_kscale(N)
    u = mx_kscale(T)
    t = mx_kscale(T)
    pu = np.random.standard_normal((N, N)) / np.sqrt(N)
    x = np.random.standard_normal((N, T))
    pt = np.random.standard_normal((T, T)) / np.sqrt(T) / T ** 0.25
    z = np.random.standard_normal((T, J))
    pt_words, pt_scales = pack4(pt * u[:, None] / t)
    z_words, z_scales = pack4(z / u[:, None])
    return {"pu": bf(pu * s),
            "x": bf(x / s[:, None]),
            "cap": bf(1.2 + 0.1 * np.random.standard_normal(N)),
            "w": bf(np.random.uniform(0.5, 1.5, T) / T ** 0.25 * t),
            "pt_words": pt_words, "pt_scales": pt_scales,
            "z_words": z_words, "z_scales": z_scales}


def reference(pu, x, cap, w, pt_words, pt_scales, z_words, z_scales):
    a = mxq(f64(pu), 1, "e4m3") @ mxq(f64(x), 0, "e4m3")
    c = f64(cap)[:, None]
    left = np.minimum(np.maximum(a, -c), c) * f64(w)
    right = unpack4(pt_words, pt_scales).T @ unpack4(z_words, z_scales)
    return mxq(left, 1, "e4m3") @ mxq(right, 0, "e4m3")

from contextlib import ExitStack

import concourse.mybir as mybir
from concourse.masks import make_identity

UNITS, PERIODS, INSTR = 1024, 1536, 512
FLOPS = 2 * (UNITS * UNITS * PERIODS + PERIODS * PERIODS * INSTR + UNITS * PERIODS * INSTR)

F32 = mybir.dt.float32
BF16 = mybir.dt.bfloat16
I32 = mybir.dt.int32
U32 = mybir.dt.uint32
U8 = mybir.dt.uint8
FP8X4 = mybir.dt.float8_e4m3fn_x4
FP4X4 = mybir.dt.float4_e2m1fn_x4
ALU = mybir.AluOpType

P = 128
KP = 512
NT = UNITS // P
SP = UNITS // KP
G = PERIODS // KP
JT = INSTR // P
PAIRS = NT // 2
BATCHES = ((0,0,4),(0,4,4),(1,0,4),(1,4,4),(2,0,4),(2,4,2),(2,6,1),(2,7,1))
ORDER = """mp.0.1 id lpu.2.4 mz lx.1.1 put.3 wy put.2 lx.1.0 lpu.0.2 mp.1.3 xv.1.1.0.1 wt.0 lx.0.1 lx.0.0 lpu.4.8 xv.1.1.1.1 puw.3 puw.2 xv.1.0.1.1 cg xs.1.0.0.1 wt.1 puq.2.2 zy caps ws.1 put.0 xq.1.0.2 put.1 lx.2.0 xv.0.1.0.1 am.2.3 lpt.0.1 puw.0 puq.0.1 am.2.2 xv.0.0.1.1 xs.0.1.1.1 xs.0.0.0.1 xq.0.1.1 am.2.0 put.5 puw.1 cl.2.3 xq.0.0.1 puq.1.1 py.0.1 put.7 ws.0 puw.5 am.0.0 cl.2.2 cl.2.0 lz puw.7 put.6 put.4 xs.2.0.1.1 am.0.3 ev.2.2 lx.2.1 cl.0.0 ps.0 eg.2.3 am.2.1 am.0.1 rm.0.0 puw.4 cl.0.3 cl.2.1 lpt.1.3 puw.6 rm.0.2 cl.0.1 py.1.3 puq.6.2 xs.2.0.0.1 eg.0.0 rr.0.0 am.0.2 puq.4.2 am.3.3 xs.2.1.1.1 ev.2.1 ev.2.0 rm.0.1 rr.0.2 cl.0.2 rr.0.1 xs.2.1.0.1 am.3.1 ps.1 eg.0.1 lt.2.1 lw.2.1 cl.3.3 lt.0.0 rm.0.3 lw.0.0 eg.0.2 cl.3.1 am.1.1 ev.0.3 rm.1.1 lt.0.1 rr.0.3 xq.2.0.2 lt.2.0 am.3.0 cl.1.1 rr.1.1 ps.2 lw.0.1 rm.1.2 is.0.1 am.1.3 am.3.2 rm.1.3 cl.3.0 rr.1.2 is.0.0 rm.1.0 rr.1.3 ev.3.1 rr.1.0 lw.2.0 cl.1.3 cl.3.2 am.1.2 am.1.0 rm.2.1 ev.3.0 rm.2.3 ev.3.2 is.1.1 cl.1.2 cl.1.0 rr.2.3 am.4.3 ru.2.1 eg.1.1 rm.2.0 eg.3.3 eg.1.3 eg.1.2 ev.1.0 lt.3.0 wt.2 is.1.0 cl.4.3 rm.2.2 lq.2 lq.0 rr.2.0 ws.2 am.4.0 am.4.1 rq.0 rr.2.2 am.6.0 rq.1 lw.3.0 cl.4.0 cl.4.1 cl.6.0 am.4.2 is.2.1 eg.4.3 lt.1.0 cl.4.2 ev.4.0 lt.3.1 am.7.0 ev.4.2 eg.4.1 lw.1.0 lw.3.1 am.5.0 is.2.0 cl.7.0 lt.4.0 lu.4.0 lt.4.1 eg.6.0 om.1.0.1 om.2.0.1 lw.4.1 rq.2 am.5.1 lq.4 cl.5.0 om.1.2 lt.1.1 lq.3 lt.6.0 om.2.2 ev.7.0 os.1 lw.1.1 cl.5.1 om.0.0.1 eg.5.0 os.2 om.0.2 lw.6.0 lq.1 lt.7.0 om.3.0.1 lq.6 os.0 ev.5.1 om.3.2 lw.7.0 om.6.0.1 os.3 om.6.2 lt.5.0 lq.7 lu.5.0 os.6 om.7.2 om.7.0.1 om.4.0.1 os.7 lq.5 om.4.2 os.4 om.5.0.1 om.5.2 ov.5"""


def tile_two_way_within_moment_s12_kernel(tc, pu, x, cap, w, pt_words, pt_scales, z_words, z_scales, out):
    nc = tc.nc
    with ExitStack() as ctx:
        keep = ctx.enter_context(tc.tile_pool(name="keep", bufs=1))
        work = ctx.enter_context(tc.tile_pool(name="work", bufs=3))
        ps_a = ctx.enter_context(tc.psum_pool(name="ps_a", bufs=3))
        ps_t = ctx.enter_context(tc.psum_pool(name="ps_t", bufs=2))
        ps_m = ctx.enter_context(tc.psum_pool(name="ps_m", bufs=2))
        ps_w = ctx.enter_context(tc.psum_pool(name="ps_w", bufs=1))
        ctx.enter_context(tc.manual_schedule())

        ident = keep.tile([P, P], F32)
        cap_raw = keep.tile([P, NT], BF16)
        cap_hi = keep.tile([P, NT], F32)
        cap_lo = keep.tile([P, NT], F32)
        w_raw = keep.tile([P, 2 * G, 2], BF16)
        w_bank = ps_w.tile([P, 2, 2, P], F32)
        w_all = keep.tile([P, G, KP], BF16)
        pu_raw = keep.tile([P, NT, UNITS], BF16)
        pu_woven = keep.tile([P, NT, 4 * SP * P], BF16, align_bytes=64)
        pu_codes = keep.tile([P, NT, SP, P], U32, align_bytes=64)
        pu_scale = keep.tile([P, NT, SP, P], U8, align_bytes=64)
        x_raw = keep.tile([P, G, SP, 4, KP], BF16)
        x_woven = keep.tile([P, G, SP, KP, 4], BF16, align_bytes=64)
        x_codes = keep.tile([P, G, SP, KP], U32, align_bytes=64)
        x_scale = keep.tile([P, G, SP, KP], U8, align_bytes=64)
        pt_codes = keep.tile([P, G, 2 * PERIODS], U8, align_bytes=64)
        pt_scale = keep.tile([P, G, PERIODS], U8, align_bytes=64)
        pts_codes = keep.tile([P, G, G, 2 * KP], U8, align_bytes=64)
        pts_scale = keep.tile([P, G, G, KP], U8, align_bytes=64)
        z_codes = keep.tile([P, G, 2 * INSTR], U8, align_bytes=64)
        z_scale = keep.tile([P, G, INSTR], U8, align_bytes=64)
        r_slots = keep.tile([P, G, 4, INSTR], BF16)
        r_codes = keep.tile([P, G, INSTR], U32, align_bytes=64)
        r_scale = keep.tile([P, G, INSTR], U8, align_bytes=64)
        l_codes = keep.tile([P, G, NT, P], U32, align_bytes=64)
        l_scale = keep.tile([P, G, NT, P], U8, align_bytes=64)

        pu_rows = pu.rearrange("(p i) k -> p i k", i=NT)
        out_rows = out.rearrange("(p i) j -> p i j", i=NT)
        live = {}

        def load_pu(i0, i1):
            nc.sync.dma_start(out=pu_raw[:, i0:i1, :], in_=pu_rows[:, i0:i1, :])

        def load_x(g, s):
            rows = x[KP * s : KP * (s + 1), KP * g : KP * (g + 1)]
            nc.sync.dma_start(out=x_raw[:, g, s], in_=rows.rearrange("(p j) t -> p j t", j=4))

        def load_pt(g0, g1):
            cols = slice(2 * KP * g0, 2 * KP * g1)
            nc.sync.dma_start(
                out=pt_codes[:, :, cols].bitcast(I32),
                in_=pt_words.rearrange("c p b -> p c b")[:, :, cols].bitcast(I32),
            )

        def load_scales(eng, plane, src, n0, n1):
            for r in range(4):
                eng.dma_start(
                    out=plane[r:P:32, :, n0:n1].bitcast(I32),
                    in_=src.rearrange("c (q r) n -> r q c n", r=4)[r, :, :, n0:n1].bitcast(I32),
                )

        def turn(name, sources):
            bank = ps_t.tile([P, 4, P], F32, tag="turn", name="bank")
            for m, src in enumerate(sources):
                nc.tensor.transpose(bank[:, m, :], src, ident[:])
            live[name] = bank

        def weave(name, dst, n=2, copy=nc.scalar.copy):
            bank = live.pop(name)
            copy(
                out=dst.bitcast(F32).rearrange("p (a n u) -> p a n u", a=n, u=2),
                in_=bank[:, : 2 * n].rearrange("p (a u) n -> p a n u", u=2),
            )

        def quantize(codes, scales, src):
            nc.vector.quantize_mx(out=codes.bitcast(FP8X4), scales=scales, in_=src)

        def pu_turn(i):
            words = pu_raw[:, i, :].bitcast(F32)
            turn(("pu", i), [words[:, 256 * s + u : 256 * (s + 1) : 2] for s in range(SP) for u in range(2)])

        def pu_weave(i):
            weave(("pu", i), pu_woven[:, i])

        def pu_quant(i, n):
            quantize(
                pu_codes[:, i : i + n].rearrange("p i s n -> p (i s n)"),
                pu_scale[:, i : i + n].rearrange("p i s n -> p (i s n)"),
                pu_woven[:, i : i + n].rearrange("p i n -> p (i n)"),
            )

        def x_weave(g, s, copy, c0, c1):
            copy(
                out=x_woven[:, g, s, c0:c1, :].rearrange("p (c i) j -> p c j i", i=4),
                in_=x_raw[:, g, s, :, c0:c1].rearrange("p j (c i) -> p c j i", i=4),
            )

        def x_quant(g, s, n):
            quantize(
                x_codes[:, g, s : s + n].rearrange("p s t -> p (s t)"),
                x_scale[:, g, s : s + n].rearrange("p s t -> p (s t)"),
                x_woven[:, g, s : s + n].rearrange("p s t j -> p (s t j)"),
            )

        def pt_sort(g):
            for dst, src, width in ((pts_codes, pt_codes, 2 * KP), (pts_scale, pt_scale, KP)):
                nc.vector.tensor_copy(
                    out=dst[:, g].bitcast(I32).rearrange("p c (s q v) -> p c s q v", s=4, q=16),
                    in_=src[:, :, width * g : width * (g + 1)].bitcast(I32).rearrange("p c (q s v) -> p c s q v", s=4, q=16),
                )

        def r_mm(g, s):
            acc = ps_m.tile([P, KP], F32, tag="acc_m", name="acc")
            for c in range(G):
                nc.tensor.matmul_mx(
                    out=acc[:],
                    lhsT=pts_codes[:, g, c, 2 * P * s : 2 * P * (s + 1)].bitcast(FP4X4),
                    lhsT_scale=pts_scale[:, g, c, P * s : P * (s + 1)],
                    rhs=z_codes[:, c].bitcast(FP4X4),
                    rhs_scale=z_scale[:, c],
                    start=(c == 0),
                    stop=(c == G - 1),
                )
            live["r_acc", g, s] = acc

        def r_round(g, s, copy=nc.scalar.copy):
            copy(out=r_slots[:, g, s], in_=live.pop(("r_acc", g, s))[:])

        def r_weave(g, h, copy):
            if ("r_woven", g) not in live:
                woven = work.tile([P, INSTR, 4], BF16, tag="r_woven", bufs=2, align_bytes=64)
                live["r_woven", g] = woven
            cols = slice(256 * h, 256 * (h + 1))
            copy(
                out=live["r_woven", g][:, cols, :].rearrange("p (c i) j -> p c j i", i=4),
                in_=r_slots[:, g, :, cols].rearrange("p j (c i) -> p c j i", i=4),
            )

        def r_quant(g):
            quantize(r_codes[:, g], r_scale[:, g], live.pop(("r_woven", g))[:].rearrange("p n j -> p (n j)"))

        def a_mm(k, a):
            g, i = BATCHES[k][0], BATCHES[k][1] + a
            acc = ps_a.tile([P, KP], F32, tag="acc_a", name="acc")
            for s in range(SP):
                nc.tensor.matmul_mx(
                    out=acc[:],
                    lhsT=pu_codes[:, i, s].bitcast(FP8X4),
                    lhsT_scale=pu_scale[:, i, s],
                    rhs=x_codes[:, g, s].bitcast(FP8X4),
                    rhs_scale=x_scale[:, g, s],
                    start=(s == 0),
                    stop=(s == SP - 1),
                )
            live["a_acc", k, a] = acc

        def clip(k, a):
            i = BATCHES[k][1] + a
            if ("clipped", k) not in live:
                clipped = work.tile([P, BATCHES[k][2], KP], F32, tag="clipped", bufs=2)
                live["clipped", k] = clipped
            acc = live.pop(("a_acc", k, a))
            nc.vector.tensor_scalar(
                out=live["clipped", k][:, a, :].rearrange("p (u q r e) -> p q u r e", u=2, r=8, e=2),
                in0=acc[:].rearrange("p (q u e r) -> p q u r e", u=2, r=8, e=2),
                scalar1=cap_lo[:, i : i + 1],
                scalar2=cap_hi[:, i : i + 1],
                op0=ALU.max,
                op1=ALU.min,
            )

        def sorted_view(ap):
            return ap.rearrange("p (u q r e) -> p q u r e", u=2, r=8, e=2)

        def w_view(g):
            flat = w_bank[:, g % 2].rearrange("p m n -> p (m n)").bitcast(BF16)
            return flat.rearrange("p (q u e r) -> p q u r e", u=2, r=8, e=2)

        def weigh(k, a, on_vector):
            g, i0, n = BATCHES[k]
            if ("left", k) not in live:
                left = work.tile([P, n, KP], BF16, tag="left")
                live["left", k] = left
            left, clipped = live["left", k][:, a], live["clipped", k][:, a]
            if on_vector:
                nc.vector.tensor_tensor(out=sorted_view(left), in0=sorted_view(clipped), in1=w_view(g), op=ALU.mult)
            else:
                nc.gpsimd.tensor_tensor(out=left, in0=clipped, in1=w_all[:, g], op=ALU.mult)

        def l_turn(k, h):
            n = min(2, BATCHES[k][2])
            words = live["left", k][:, 2 * h : 2 * h + n].rearrange("p a t -> p (a t)").bitcast(F32)
            turn(("l", k, h), [words[:, P * m : P * (m + 1)] for m in range(2 * n)])

        def l_weave(k, h, copy=nc.scalar.copy):
            n = min(2, BATCHES[k][2])
            if ("l_woven", k) not in live:
                woven = work.tile([P, BATCHES[k][2] * KP], BF16, tag="l_woven", align_bytes=64)
                live["l_woven", k] = woven
            weave(("l", k, h), live["l_woven", k][:, 2 * KP * h : 2 * KP * h + n * KP], n, copy)

        def l_quant(k):
            g, i0, n = BATCHES[k]
            quantize(
                l_codes[:, g, i0 : i0 + n].rearrange("p a n -> p (a n)"),
                l_scale[:, g, i0 : i0 + n].rearrange("p a n -> p (a n)"),
                live.pop(("l_woven", k))[:],
            )

        def o_mm(i, *groups):
            if ("o_acc", i) not in live:
                acc = ps_m.tile([P, KP], F32, tag="acc_m", name="acc")
                live["o_acc", i] = acc
                live["o_done", i] = 0
            for g in groups:
                nc.tensor.matmul_mx(
                    out=live["o_acc", i][:],
                    lhsT=l_codes[:, g, i].bitcast(FP8X4),
                    lhsT_scale=l_scale[:, g, i],
                    rhs=r_codes[:, g].bitcast(FP8X4),
                    rhs_scale=r_scale[:, g],
                    start=(live["o_done", i] == 0),
                    stop=(live["o_done", i] == G - 1),
                )
                live["o_done", i] += 1

        def o_store(i, copy):
            result = work.tile([P, INSTR], F32, tag="result")
            copy(out=result[:], in_=live.pop(("o_acc", i))[:])
            nc.sync.dma_start(out=out_rows[:, i, :], in_=result[:])

        def half_mm(i, h):
            acc = ps_m.tile([P, KP], F32, tag="acc_m", name="acc")
            cols = slice(256 * h, 256 * (h + 1))
            for g in range(G):
                nc.tensor.matmul_mx(
                    out=acc[:, :256],
                    lhsT=l_codes[:, g, i].bitcast(FP8X4),
                    lhsT_scale=l_scale[:, g, i],
                    rhs=r_codes[:, g, cols].bitcast(FP8X4),
                    rhs_scale=r_scale[:, g, cols],
                    start=(g == 0),
                    stop=(g == G - 1),
                )
            live["h_acc", i, h] = acc

        def half_store(i, h, copy, queue):
            result = work.tile([P, 256], F32, tag="result")
            copy(out=result[:], in_=live.pop(("h_acc", i, h))[:, :256])
            queue.dma_start(out=out_rows[:, i, 256 * h : 256 * (h + 1)], in_=result[:])

        vcopy, scopy = nc.vector.tensor_copy, nc.scalar.copy
        w_words = w_raw[:].rearrange("p m e -> p (m e)").bitcast(F32)

        def w_turn(g):
            for m in range(2):
                src = w_words[:, 2 * g + m : 2 * g + m + 1].to_broadcast([P, P])
                nc.tensor.transpose(w_bank[:, g % 2, m, :], src, ident[:])

        def w_sort(g):
            nc.scalar.copy(out=sorted_view(w_all[:, g]), in_=w_view(g))

        def caps():
            nc.vector.tensor_copy(out=cap_hi[:], in_=cap_raw[:])
            nc.vector.tensor_scalar(out=cap_lo[:], in0=cap_raw[:], scalar1=-1.0, scalar2=None, op0=ALU.mult)

        def load_z(c0=0, c1=G):
            nc.sync.dma_start(
                out=z_codes[:, c0:c1].bitcast(I32), in_=z_words.rearrange("c p b -> p c b")[:, c0:c1].bitcast(I32)
            )

        def warm(n):
            acc = ps_m.tile([P, KP], F32, tag="acc_m", name="acc")
            for rep in range(2):
                nc.tensor.matmul_mx(
                    out=acc[:],
                    lhsT=z_codes[:, 0, : 2 * P].bitcast(FP4X4),
                    lhsT_scale=z_scale[:, 0, :P],
                    rhs=z_codes[:, 0].bitcast(FP4X4),
                    rhs_scale=z_scale[:, 0],
                    start=True,
                    stop=True,
                )

        def gcopy(out, in_):
            nc.gpsimd.tensor_scalar(out=out, in0=in_, scalar1=1.0, scalar2=1.0, op0=ALU.mult, op1=ALU.mult)

        tasks = {
            "mz": lambda: nc.vector.memset(z_scale[:].bitcast(I32), 0),
            "mp": lambda g0, g1: nc.vector.memset(pt_scale[:, :, KP * g0 : KP * g1].bitcast(I32), 0),
            "du": warm, "id": lambda: make_identity(nc, ident[:]),
            "hm": half_mm, "hv": lambda i, h: half_store(i, h, vcopy, nc.sync), "hs": lambda i, h: half_store(i, h, scopy, nc.scalar),
            "xg": lambda g, s, h, n: x_weave(g, s, gcopy, 256 * h, 256 * (h + n)),
            "ig": lambda g, h: r_weave(g, h, gcopy),
            "lu": lambda k, h: l_weave(k, h, vcopy), "ru": lambda g, s: r_round(g, s, vcopy),
            "lpu": load_pu, "lx": load_x, "lpt": load_pt, "lz": load_z,
            "zy": lambda: load_scales(nc.sync, z_scale, z_scales, 0, INSTR),
            "zg": lambda: load_scales(nc.gpsimd, z_scale, z_scales, 0, INSTR),
            "py": lambda g0, g1: load_scales(nc.sync, pt_scale, pt_scales, KP * g0, KP * g1),
            "pg": lambda g0, g1: load_scales(nc.gpsimd, pt_scale, pt_scales, KP * g0, KP * g1),
            "wy": lambda: nc.sync.dma_start(out=w_raw[:], in_=w.rearrange("(m p e) -> p m e", p=P, e=2)),
            "wg": lambda: nc.gpsimd.dma_start(out=w_raw[:], in_=w.rearrange("(m p e) -> p m e", p=P, e=2)),
            "cy": lambda: nc.sync.dma_start(out=cap_raw[:], in_=cap.rearrange("(p i) -> p i", i=NT)),
            "cg": lambda: nc.gpsimd.dma_start(out=cap_raw[:], in_=cap.rearrange("(p i) -> p i", i=NT)),
            "wt": w_turn, "caps": caps,
            "put": pu_turn, "puw": pu_weave, "puq": pu_quant,
            "xv": lambda g, s, h, n: x_weave(g, s, vcopy, 256 * h, 256 * (h + n)),
            "xs": lambda g, s, h, n: x_weave(g, s, scopy, 256 * h, 256 * (h + n)),
            "xq": x_quant,
            "rm": r_mm, "rr": r_round, "rq": r_quant, "ps": pt_sort, "ws": w_sort,
            "iv": lambda g, h: r_weave(g, h, vcopy), "is": lambda g, h: r_weave(g, h, scopy),
            "am": a_mm, "cl": clip, "ev": lambda k, a: weigh(k, a, True), "eg": lambda k, a: weigh(k, a, False), "lt": l_turn, "lw": l_weave, "lq": l_quant,
            "om": o_mm, "ov": lambda i: o_store(i, vcopy), "os": lambda i: o_store(i, scopy),
        }
        for item in ORDER.split():
            name, *args = item.split(".")
            tasks[name](*map(int, args))
